import numpy as np
import ml_dtypes


def mxq(x, axis, fmt="e4m3"):
    dtype, down = {"e4m3": (ml_dtypes.float8_e4m3fn, 7), "e5m2": (ml_dtypes.float8_e5m2, 14)}[fmt]
    v = np.moveaxis(np.asarray(x, np.float32).astype(ml_dtypes.bfloat16).astype(np.float64), axis, -1)
    blocks = v.reshape(v.shape[:-1] + (-1, 32))
    amax = np.abs(blocks).max(-1, keepdims=True)
    byte = np.maximum(np.where(amax > 0, np.frexp(amax)[1] - 1 + 127, 0) - down, 1)
    scale = np.exp2(byte - 127.0)
    codes = (blocks / scale).astype(np.float32).astype(dtype).astype(np.float64)
    return np.moveaxis((codes * scale).reshape(v.shape), -1, axis)


WIDE = False


def mx_kscale(k):
    if not WIDE:
        return np.ones(k)
    levels = np.array([10, -10, 5, -5, 0])
    if k % 512:
        return np.exp2(np.random.permutation(np.resize(levels, k // 32))).repeat(32)
    a = np.empty((k // 512, 16))
    for p in range(k // 512):
        a[p, :8] = np.random.permutation(np.resize(levels, 8))
        for g in range(8):
            far = levels[np.abs(levels - a[p, g]) >= 10]
            a[p, g + 8] = far[np.random.randint(len(far))]
    return np.exp2(a.ravel()).repeat(32)


def f64(x):
    return np.asarray(x).astype(np.float64)


def striped(idx):
    return np.tile(idx.reshape(-1, 16).T, (8, 1)).astype(np.uint16)


def unstriped(offs):
    return offs[:16].T.reshape(-1).astype(np.int64)


E2M1 = np.array([0.0, 0.5, 1.0, 1.5, 2.0, 3.0, 4.0, 6.0, -0.0, -0.5, -1.0, -1.5, -2.0, -3.0, -4.0, -6.0])


def pack_weight(w, fmt):
    k, n = w.shape
    w = f64(np.asarray(w, np.float32).astype(ml_dtypes.bfloat16)).reshape(k // 32, 32, n)
    amax = np.abs(w).max(1)
    if fmt == "e4m3":
        byte = np.frexp(amax)[1] - 1 + 127 - 7
    else:
        mant, ex = np.frexp(amax / 6.0)
        byte = np.where(mant > 0.5, ex, ex - 1) + 127
    byte = np.clip(np.where(amax > 0, byte, 1), 1, 254)
    scaled = (w * np.exp2(127.0 - byte)[:, None, :]).reshape(k, n).astype(np.float32)
    by_word = np.ascontiguousarray(scaled.reshape(k // 512, 128, 4, n).transpose(0, 1, 3, 2))
    if fmt == "e4m3":
        words = by_word.astype(ml_dtypes.float8_e4m3fn).view(np.uint8)
    else:
        c = by_word.astype(ml_dtypes.float4_e2m1fn).view(np.uint8) & 0xF
        words = (c[..., 0::2] | (c[..., 1::2] << 4)).reshape(k // 512, 128, 2 * n)
    return np.ascontiguousarray(words), np.ascontiguousarray(byte.astype(np.uint8).reshape(k // 512, 16, n))


def unpack_weight(words, scales, fmt):
    g, _, n = scales.shape
    words = np.ascontiguousarray(words).reshape(g, 128, n, -1)
    if fmt == "e4m3":
        vals = words.view(ml_dtypes.float8_e4m3fn).astype(np.float64)
    else:
        nib = np.empty((g, 128, n, 4), np.uint8)
        nib[..., 0::2] = words & 0xF
        nib[..., 1::2] = words >> 4
        vals = E2M1[nib]
    vals = vals * np.repeat(np.exp2(scales.astype(np.float64) - 127.0), 8, axis=1)[..., None]
    return vals.transpose(0, 1, 3, 2).reshape(g * 512, n)


K, T, E, C = 512, 512, 4, 256


def deal():
    first = np.random.permutation(np.repeat(np.arange(E), T // E))
    second = (first + 1 + np.random.permutation(np.repeat(np.arange(E - 1), -(-T // (E - 1)))[:T])) % E
    while np.bincount(second, minlength=E).max() != T // E:
        load = np.bincount(second, minlength=E); hi, lo = int(load.argmax()), int(load.argmin())
        t = np.flatnonzero((second == hi) & (first != lo))[0]; second[t] = lo
    slot_token = np.empty(E * C, np.int64); pos = np.empty((2, T), np.int64); fill = np.zeros(E, np.int64)
    place = np.stack([np.random.permutation(C) for _ in range(E)])
    for r, deal in enumerate((first, second)):
        for t in np.random.permutation(T):
            e = deal[t]; j = e * C + place[e, fill[e]]; fill[e] += 1; slot_token[j] = t; pos[r, t] = j
    g = np.random.uniform(0.2, 0.8, T)
    return slot_token, pos, np.stack([g, 1.0 - g])


def by_expert(wq, xq):
    return np.concatenate([wq[e].T @ xq[:, e * C:(e + 1) * C] for e in range(E)], axis=1)


def setup_inputs():
    n = np.random.standard_normal
    s = mx_kscale(K)
    slots1, pos1, g1 = deal()
    slots2, pos2, g2 = deal()
    x = pack_weight(n((K, T)) * s[:, None], "e4m3")
    return {
        "x_words": x[0],
        "x_scales": x[1],
        "w": (n((E, K, K)) / np.sqrt(K) / s[None, :, None] * s).astype(np.float32),
        "gate1": (np.stack([np.tile(r, (128, 1)) for r in g1])).astype(np.float32),
        "gate2": (np.stack([np.tile(r, (128, 1)) for r in g2])).astype(np.float32),
        "offs": striped(slots1),
        "pos1": striped(pos1[0]),
        "pos2": striped(pos1[1]),
        "offs2": striped(slots2),
        "pos3": striped(pos2[0]),
        "pos4": striped(pos2[1]),
    }


def reference(x_words, x_scales, w, gate1, gate2, offs, pos1, pos2, offs2, pos3, pos4):
    wq = mxq(f64(w), 1, "e4m3")
    idx, idx2 = unstriped(offs), unstriped(offs2)
    y = by_expert(wq, unpack_weight(x_words, x_scales, "e4m3")[:, idx])
    c = sum(f64(gate1[r, :1]) * y[:, unstriped(p)] for r, p in enumerate((pos1, pos2)))
    z = by_expert(wq, mxq(c[:, idx2], 0, "e4m3"))
    out = sum(f64(gate2[r, :1]) * z[:, unstriped(p)] for r, p in enumerate((pos3, pos4)))
    return out

@@ -1,0 +1,291 @@
+from contextlib import ExitStack
+
+import concourse.mybir as mybir
+from concourse.masks import make_identity
+
+K, T, E, C = 512, 512, 4, 256
+S = E * C
+P = 128
+FLOPS = 2 * 2 * K * K * S
+
+F32 = mybir.dt.float32
+BF16 = mybir.dt.bfloat16
+I32 = mybir.dt.int32
+U32 = mybir.dt.uint32
+U16 = mybir.dt.uint16
+U8 = mybir.dt.uint8
+FP8X4 = mybir.dt.float8_e4m3fn_x4
+MULT = mybir.AluOpType.mult
+ADD = mybir.AluOpType.add
+COPY = mybir.ActivationFunctionType.Copy
+
+VECTOR_CASTS = ((2, 1), (3, 0), (3, 1))
+TURNED1 = ((0, 0), (0, 1), (0, 2), (0, 3), (1, 0), (1, 1))
+PLAIN1 = ((1, 256, 256),)
+TURNED2 = ((0, 0), (0, 1), (0, 2), (0, 3), (1, 0), (1, 1))
+PLAIN2 = ((1, 256, 256),)
+
+
+def entries(lst, first, count):
+    return lst[:, first // 16 : (first + count) // 16]
+
+
+def tile_moe_uni_none_kernel(
+    tc, x_words, x_scales, w, gate1, gate2, offs, pos1, pos2, offs2, pos3, pos4, out
+):
+    nc = tc.nc
+    with ExitStack() as ctx:
+        keep = ctx.enter_context(tc.tile_pool(name="keep", bufs=1))
+        late_psum = ctx.enter_context(tc.psum_pool(name="late_psum", bufs=4))
+        fw_psum = ctx.enter_context(tc.psum_pool(name="fw_psum", bufs=2))
+        acc_psum = ctx.enter_context(tc.psum_pool(name="acc_psum", bufs=2))
+
+        def load_list(src, name):
+            t = keep.tile(list(src.shape), U16, name=name)
+            nc.sync.dma_start(t[:], src)
+            return t
+
+        def load_w(e, h):
+            raw = keep.tile([P, 4, 256], F32, name="w_raw%d%d" % (e, h))
+            nc.sync.dma_start(raw[:], w[e].rearrange("(p j) n -> p j n", j=4)[:, :, 256 * h : 256 * (h + 1)])
+            return raw
+
+        def load_wide(gate, plain, name):
+            first = min(f for u, f, n in plain)
+            wide = keep.tile([P, 2, T - first], F32, name=name)
+            nc.sync.dma_start(wide[:], gate.rearrange("r p t -> p r t")[:, :, first:T])
+            return wide, first
+
+        x_planes = keep.tile([P, T], U8, name="x_planes", align_bytes=64)
+        nc.vector.memset(x_planes[:].bitcast(I32), 0)
+        ident = keep.tile([P, P], F32, name="ident")
+        make_identity(nc, ident[:])
+        gate_rows = keep.tile([P, P], F32, name="gate_rows")
+        nc.scalar.activation(gate_rows[:], ident[:], COPY, scale=0.0)
+
+        offs_sb = load_list(offs, "offs_sb")
+        x_sb = keep.tile([P, T], I32, name="x_sb", align_bytes=64)
+        nc.sync.dma_start(x_sb[:], x_words[0].rearrange("p t d -> p (t d)").bitcast(I32))
+        w_raw = {(0, 0): load_w(0, 0)}
+        pos1_sb = load_list(pos1, "pos1_sb")
+        scale_rows = x_scales[0].rearrange("(q r) t -> r q t", r=4)
+        for r in range(4):
+            nc.sync.dma_start(x_planes[r:P:32, :].bitcast(I32), scale_rows[r].bitcast(I32))
+        for e in range(E):
+            for h in range(2):
+                if (e, h) != (0, 0):
+                    w_raw[e, h] = load_w(e, h)
+        pos2_sb = load_list(pos2, "pos2_sb")
+        for n, gate in enumerate((gate1, gate2)):
+            rows = gate.rearrange("r p (c n) -> (r p c) n", n=P)
+            nc.sync.dma_start(gate_rows[8 * n : 8 * n + 8, :], rows[508:516, :])
+        wide1 = load_wide(gate1, PLAIN1, "wide1")
+        offs2_sb = load_list(offs2, "offs2_sb")
+        pos3_sb = load_list(pos3, "pos3_sb")
+        pos4_sb = load_list(pos4, "pos4_sb")
+        wide2 = load_wide(gate2, PLAIN2, "wide2")
+
+        x_codes, x_sc, w_bf, w_codes, w_sc = {}, {}, {}, {}, {}
+
+        def fetch_x_words(e):
+            x_codes[e] = keep.tile([P, C], U32, name="x_codes%d" % e, align_bytes=64)
+            nc.vector.tensor_copy(x_codes[e][:], x_sb[:].bitcast(U32).indirect(entries(offs_sb, e * C, C)))
+
+        def fetch_x_scales(first_e, tag):
+            both = keep.tile([P, 2, C], U8, name="x_sc%d" % first_e, tag=tag, align_bytes=64)
+            for n in range(2):
+                x_sc[first_e + n] = both[:, n, :]
+                nc.vector.tensor_copy(both[:, n, :], x_planes[:].indirect(entries(offs_sb, (first_e + n) * C, C)))
+
+        def cast_w(e, h):
+            if h == 0:
+                w_bf[e] = keep.tile([P, 4, P, 4], BF16, name="w_bf%d" % e, tag="w_bf%d" % e, align_bytes=64)
+            dst = w_bf[e][:, :, 64 * h : 64 * (h + 1), :].rearrange("p t m j -> p m j t")
+            src = w_raw[e, h][:].rearrange("p j (m t) -> p m j t", t=4)
+            if (e, h) in VECTOR_CASTS:
+                nc.vector.tensor_copy(dst, src)
+            else:
+                nc.scalar.copy(dst, src)
+
+        def quantize_w(e, pairs):
+            if pairs[0] == 0:
+                w_codes[e] = keep.tile([P, K], U32, name="w_codes%d" % e, align_bytes=64)
+                w_sc[e] = keep.tile([P, K], U8, name="w_sc%d" % e, align_bytes=64)
+            cols = slice(256 * pairs[0], 256 * (pairs[-1] + 1))
+            src = w_bf[e][:, 2 * pairs[0] : 2 * pairs[-1] + 2, :, :].rearrange("p t m j -> p (t m j)")
+            nc.vector.quantize_mx(w_codes[e][:, cols].bitcast(FP8X4), w_sc[e][:, cols], src)
+
+        def multiply(e, u, codes, scales, count):
+            if u == 0:
+                bank = acc_psum.tile([P, 2, 256], F32, name="acc_bank")
+            else:
+                bank = late_psum.tile([P, 2, 256], F32, name="late_bank")
+            for b in range(2):
+                cols = slice(P * (2 * u + b), P * (2 * u + b + 1))
+                nc.tensor.matmul_mx(
+                    out=bank[:, b, 0:count],
+                    lhsT=w_codes[e][:, cols].bitcast(FP8X4),
+                    lhsT_scale=w_sc[e][:, cols],
+                    rhs=codes.bitcast(FP8X4),
+                    rhs_scale=scales,
+                    start=True,
+                    stop=True,
+                )
+            return bank
+
+        def empty(bank, u, first, count, results, on_vector=False):
+            for b in range(2):
+                copy = nc.vector.tensor_copy if on_vector else nc.scalar.copy
+                copy(results[2 * u + b][:, first : first + count], bank[:, b, 0:count])
+
+        y = [keep.tile([P, S], F32, name="y%d" % j) for j in range(2)]
+        for e in range(E):
+            fetch_x_words(e)
+        fetch_x_scales(0, "x_sc0")
+        late = []
+        for e in range(E):
+            cast_w(e, 0)
+            cast_w(e, 1)
+            if e < E - 1:
+                quantize_w(e, (0, 1))
+            else:
+                quantize_w(e, (0,))
+                quantize_w(e, (1,))
+            if e == 0:
+                fetch_x_scales(2, "w_bf0")
+            bank = multiply(e, 0, x_codes[e][:], x_sc[e], C)
+            late.append(multiply(e, 1, x_codes[e][:], x_sc[e], C))
+            empty(bank, 0, e * C, C, y, e == E - 1)
+        y.extend(keep.tile([P, S], F32, name="y%d" % (2 + h), tag="w_bf%d" % (2 + h), align_bytes=64) for h in range(2))
+        for e in range(E):
+            empty(late[e], 1, e * C, C, y)
+
+        gate_bank = fw_psum.tile([P, 2, 256], F32, name="fw_bank")
+        nc.tensor.transpose(gate_bank[:, 0, 0:P], gate_rows[:], ident[:])
+        gate_cols = keep.tile([P, 16], F32, name="gate_cols")
+        nc.scalar.copy(gate_cols[:], gate_bank[:, 0, 0:16])
+
+        def fetch_and_gate(step, results, lists, u, chunk):
+            bank = fw_psum.tile([P, 2, 256], F32, name="fw_bank")
+            for r in range(2):
+                got = keep.tile([P, 2, P], F32, name="got%d%d%d%d" % (step, r, u, chunk))
+                for b in range(2):
+                    nc.vector.tensor_copy(got[:, b, :], results[2 * u + b][:].indirect(entries(lists[r], P * chunk, P)))
+                    nc.tensor.transpose(bank[:, r, P * b : P * (b + 1)], got[:, b, :], ident[:])
+            gated = keep.tile([P, 2, 256], F32, name="gated%d%d%d" % (step, u, chunk))
+            for r in range(2):
+                col = 8 * step + 4 * r + chunk
+                nc.scalar.activation(gated[:, r, :], bank[:, r, :], COPY, scale=gate_cols[:, col : col + 1])
+            return gated
+
+        def turn_back(gated):
+            summed = acc_psum.tile([P, 2, 256], F32, name="acc_bank")
+            for b in range(2):
+                for r in range(2):
+                    nc.tensor.matmul(
+                        summed[:, b, 0:P],
+                        gated[:, r, P * b : P * (b + 1)],
+                        ident[:],
+                        start=(r == 0),
+                        stop=(r == 1),
+                        is_transpose=True,
+                    )
+            return summed[:, :, 0:P]
+
+        def combine_turned(step, results, lists, units, finish):
+            waiting = None
+            for u, chunk in units:
+                gated = fetch_and_gate(step, results, lists, u, chunk)
+                if waiting is not None:
+                    finish(waiting[0], waiting[1], turn_back(waiting[2]))
+                waiting = (u, chunk, gated)
+            finish(waiting[0], waiting[1], turn_back(waiting[2]))
+
+        def gated_products(step, results, lists, wide, u, first, count):
+            gates, gate_first = wide
+            prods = [keep.tile([P, 2, count], F32, name="prod%d%d%d_%d" % (step, r, u, first)) for r in range(2)]
+            for b in range(2):
+                for r in range(2):
+                    nc.vector.tensor_tensor(
+                        prods[r][:, b, :],
+                        results[2 * u + b][:].indirect(entries(lists[r], first, count)),
+                        gates[:, r, first - gate_first : first - gate_first + count],
+                        MULT,
+                    )
+            return prods
+
+        c_pairs = [keep.tile([P, T, 2], BF16, name="c_pairs%d" % u) for u in range(2)]
+
+        def round_c(u, chunk, summed):
+            nc.scalar.copy(c_pairs[u][:, P * chunk : P * (chunk + 1), :], summed.rearrange("p b t -> p t b"))
+
+        combine_turned(0, y, (pos1_sb, pos2_sb), TURNED1, round_c)
+        for u, first, count in PLAIN1:
+            prods = gated_products(0, y, (pos1_sb, pos2_sb), wide1, u, first, count)
+            nc.vector.tensor_tensor(
+                c_pairs[u][:, first : first + count, :].rearrange("p (c i) b -> p c b i", i=4),
+                prods[0][:].rearrange("p b (c i) -> p c b i", i=4),
+                prods[1][:].rearrange("p b (c i) -> p c b i", i=4),
+                ADD,
+            )
+        c_words = [c_pairs[u][:].rearrange("p t b -> p (t b)").bitcast(U32) for u in range(2)]
+
+        z = [keep.tile([P, S], F32, name="z%d" % j) for j in range(2)]
+        c_codes, c_sc, woven = {}, {}, {}
+
+        def fetch_slots(first, count, direct=False, tag=None):
+            name = "woven%d" % first
+            woven[first] = keep.tile([P, count, 2], U32, name=name, tag=(direct and tag) or name, align_bytes=64)
+            if direct:
+                for u in range(2):
+                    nc.vector.tensor_copy(woven[first][:, :, u], c_words[u].indirect(entries(offs2_sb, first, count)))
+            else:
+                name = "pairs%d" % first
+                pairs = keep.tile([P, 2, count], U32, name=name, tag=tag or name, align_bytes=64)
+                for u in range(2):
+                    nc.vector.tensor_copy(pairs[:, u, :], c_words[u].indirect(entries(offs2_sb, first, count)))
+                nc.scalar.copy(woven[first][:].bitcast(F32), pairs[:].bitcast(F32).rearrange("p u s -> p s u"))
+
+        def quantize_slots(first, count, on_vector=False):
+            c_codes[first] = keep.tile([P, count], U32, name="c_codes%d" % first, align_bytes=64)
+            c_sc[first] = keep.tile([P, count], U8, name="c_sc%d" % first, align_bytes=64)
+            nc.vector.quantize_mx(
+                c_codes[first][:].bitcast(FP8X4),
+                c_sc[first][:],
+                woven[first][:].rearrange("p s u -> p (s u)").bitcast(BF16),
+            )
+            bank = multiply(first // C, 0, c_codes[first][:], c_sc[first][:], count)
+            empty(bank, 0, first, count, z, on_vector)
+
+        fetch_slots(0, 256)
+        fetch_slots(256, 256)
+        quantize_slots(0, 256)
+        fetch_slots(512, 256, False, "woven0")
+        quantize_slots(256, 256)
+        fetch_slots(768, P, False, "woven256")
+        quantize_slots(512, 256)
+        fetch_slots(896, P, True, "woven512")
+        quantize_slots(768, P, True)
+        quantize_slots(896, P, True)
+        z.append(keep.tile([P, S], F32, name="z2", tag="woven768", align_bytes=64))
+        z.append(keep.tile([P, S], F32, name="z3", tag="woven512", align_bytes=64))
+        for first, count in ((0, 256), (256, 256), (512, 256), (768, P), (896, P)):
+            bank = multiply(first // C, 1, c_codes[first][:], c_sc[first][:], count)
+            empty(bank, 1, first, count, z)
+
+        out_planes = out.rearrange("(p j) t -> p j t", j=4)
+        staged = [keep.tile([P, 2, T], F32, name="staged%d" % u) for u in range(2)]
+
+        def store(u, chunk, summed):
+            nc.scalar.copy(staged[u][:, :, P * chunk : P * (chunk + 1)], summed)
+            if chunk % 2 == 1 or (u, chunk) == TURNED2[-1]:
+                tokens = slice(P * (chunk - chunk % 2), P * (chunk + 1))
+                nc.scalar.dma_start(out_planes[:, 2 * u : 2 * u + 2, tokens], staged[u][:, :, tokens])
+
+        combine_turned(1, z, (pos3_sb, pos4_sb), TURNED2, store)
+        for u, first, count in PLAIN2:
+            prods = gated_products(1, z, (pos3_sb, pos4_sb), wide2, u, first, count)
+            for b in range(2):
+                total = keep.tile([P, count], F32, name="total%d%d_%d" % (u, b, first))
+                nc.vector.tensor_tensor(total[:], prods[0][:, b, :], prods[1][:, b, :], ADD)
+                nc.sync.dma_start(out_planes[:, 2 * u + b, first : first + count], total[:])

@@ -1,4 +1,5 @@
 from contextlib import ExitStack
+from functools import partial
 
 import concourse.mybir as mybir
 from concourse.masks import make_identity
@@ -19,11 +20,10 @@ MULT = mybir.AluOpType.mult
 ADD = mybir.AluOpType.add
 COPY = mybir.ActivationFunctionType.Copy
 
-VECTOR_CASTS = ((2, 1), (3, 0), (3, 1))
-TURNED1 = ((0, 0), (0, 1), (0, 2), (0, 3), (1, 0), (1, 1))
-PLAIN1 = ((1, 256, 256),)
-TURNED2 = ((0, 0), (0, 1), (0, 2), (0, 3), (1, 0), (1, 1))
-PLAIN2 = ((1, 256, 256),)
+LAST = E - 1
+UNITS1 = ((0,0,256),(0,256,256),(1,0,512),(2,0,256),(3,0,256))
+UNITS2 = ((0,0,256),(0,256,256),(1,0,256),(1,256,256),(2,0,256),(2,256,256))
+SCALAR_SHARE = (128, 64, 48, 64)
 
 
 def entries(lst, first, count):
@@ -36,25 +36,24 @@ def tile_moe_uni_none_kernel(
     nc = tc.nc
     with ExitStack() as ctx:
         keep = ctx.enter_context(tc.tile_pool(name="keep", bufs=1))
-        late_psum = ctx.enter_context(tc.psum_pool(name="late_psum", bufs=4))
-        fw_psum = ctx.enter_context(tc.psum_pool(name="fw_psum", bufs=2))
-        acc_psum = ctx.enter_context(tc.psum_pool(name="acc_psum", bufs=2))
+        fw_psum = ctx.enter_context(tc.psum_pool(name="fw_psum", bufs=3))
+        acc_psum = ctx.enter_context(tc.psum_pool(name="acc_psum", bufs=5))
 
         def load_list(src, name):
             t = keep.tile(list(src.shape), U16, name=name)
             nc.sync.dma_start(t[:], src)
             return t
 
-        def load_w(e, h):
-            raw = keep.tile([P, 4, 256], F32, name="w_raw%d%d" % (e, h))
-            nc.sync.dma_start(raw[:], w[e].rearrange("(p j) n -> p j n", j=4)[:, :, 256 * h : 256 * (h + 1)])
+        def load_w(e, rows):
+            name = "w_raw%d%d" % (e, rows[0])
+            raw = keep.tile([P, len(rows), K], F32, name=name, tag=name, align_bytes=64)
+            nc.sync.dma_start(raw[:], w[e].rearrange("(p j) n -> p j n", j=4)[:, rows[0] : rows[-1] + 1, :])
             return raw
 
-        def load_wide(gate, plain, name):
-            first = min(f for u, f, n in plain)
+        def load_wide(gate, first, name):
             wide = keep.tile([P, 2, T - first], F32, name=name)
             nc.sync.dma_start(wide[:], gate.rearrange("r p t -> p r t")[:, :, first:T])
-            return wide, first
+            return wide
 
         x_planes = keep.tile([P, T], U8, name="x_planes", align_bytes=64)
         nc.vector.memset(x_planes[:].bitcast(I32), 0)
@@ -66,24 +65,21 @@ def tile_moe_uni_none_kernel(
         offs_sb = load_list(offs, "offs_sb")
         x_sb = keep.tile([P, T], I32, name="x_sb", align_bytes=64)
         nc.sync.dma_start(x_sb[:], x_words[0].rearrange("p t d -> p (t d)").bitcast(I32))
-        w_raw = {(0, 0): load_w(0, 0)}
         pos1_sb = load_list(pos1, "pos1_sb")
         scale_rows = x_scales[0].rearrange("(q r) t -> r q t", r=4)
         for r in range(4):
             nc.sync.dma_start(x_planes[r:P:32, :].bitcast(I32), scale_rows[r].bitcast(I32))
-        for e in range(E):
-            for h in range(2):
-                if (e, h) != (0, 0):
-                    w_raw[e, h] = load_w(e, h)
+        w_raw = [load_w(e, range(4)) for e in range(LAST)]
+        last_raw = [load_w(LAST, range(2)), load_w(LAST, range(2, 4))]
         pos2_sb = load_list(pos2, "pos2_sb")
         for n, gate in enumerate((gate1, gate2)):
             rows = gate.rearrange("r p (c n) -> (r p c) n", n=P)
             nc.sync.dma_start(gate_rows[8 * n : 8 * n + 8, :], rows[508:516, :])
-        wide1 = load_wide(gate1, PLAIN1, "wide1")
+        wide1 = load_wide(gate1, 256, "wide1")
         offs2_sb = load_list(offs2, "offs2_sb")
         pos3_sb = load_list(pos3, "pos3_sb")
         pos4_sb = load_list(pos4, "pos4_sb")
-        wide2 = load_wide(gate2, PLAIN2, "wide2")
+        wide2 = load_wide(gate2, 0, "wide2")
 
         x_codes, x_sc, w_bf, w_codes, w_sc = {}, {}, {}, {}, {}
 
@@ -97,40 +93,35 @@ def tile_moe_uni_none_kernel(
                 x_sc[first_e + n] = both[:, n, :]
                 nc.vector.tensor_copy(both[:, n, :], x_planes[:].indirect(entries(offs_sb, (first_e + n) * C, C)))
 
-        def cast_w(e, h):
-            if h == 0:
-                w_bf[e] = keep.tile([P, 4, P, 4], BF16, name="w_bf%d" % e, tag="w_bf%d" % e, align_bytes=64)
-            dst = w_bf[e][:, :, 64 * h : 64 * (h + 1), :].rearrange("p t m j -> p m j t")
-            src = w_raw[e, h][:].rearrange("p j (m t) -> p m j t", t=4)
-            if (e, h) in VECTOR_CASTS:
-                nc.vector.tensor_copy(dst, src)
-            else:
-                nc.scalar.copy(dst, src)
+        def cast_w(copy, e, raw, rows, planes, ms):
+            dst = w_bf[e][:, planes, ms, rows].rearrange("p t m j -> p m j t")
+            src = raw[:].rearrange("p j (m t) -> p m j t", t=4)[:, ms, :, planes]
+            copy(dst, src)
 
-        def quantize_w(e, pairs):
-            if pairs[0] == 0:
+        def quantize_w(e, first, last):
+            if first == 0:
                 w_codes[e] = keep.tile([P, K], U32, name="w_codes%d" % e, align_bytes=64)
                 w_sc[e] = keep.tile([P, K], U8, name="w_sc%d" % e, align_bytes=64)
-            cols = slice(256 * pairs[0], 256 * (pairs[-1] + 1))
-            src = w_bf[e][:, 2 * pairs[0] : 2 * pairs[-1] + 2, :, :].rearrange("p t m j -> p (t m j)")
+            cols = slice(P * first, P * last)
+            src = w_bf[e][:, first:last, :, :].rearrange("p t m j -> p (t m j)")
             nc.vector.quantize_mx(w_codes[e][:, cols].bitcast(FP8X4), w_sc[e][:, cols], src)
 
+        def one_plane(dst, e, plane, codes, scales):
+            cols = slice(P * plane, P * (plane + 1))
+            nc.tensor.matmul_mx(
+                out=dst,
+                lhsT=w_codes[e][:, cols].bitcast(FP8X4),
+                lhsT_scale=w_sc[e][:, cols],
+                rhs=codes.bitcast(FP8X4),
+                rhs_scale=scales,
+                start=True,
+                stop=True,
+            )
+
         def multiply(e, u, codes, scales, count):
-            if u == 0:
-                bank = acc_psum.tile([P, 2, 256], F32, name="acc_bank")
-            else:
-                bank = late_psum.tile([P, 2, 256], F32, name="late_bank")
+            bank = acc_psum.tile([P, 2, 256], F32, name="acc_bank")
             for b in range(2):
-                cols = slice(P * (2 * u + b), P * (2 * u + b + 1))
-                nc.tensor.matmul_mx(
-                    out=bank[:, b, 0:count],
-                    lhsT=w_codes[e][:, cols].bitcast(FP8X4),
-                    lhsT_scale=w_sc[e][:, cols],
-                    rhs=codes.bitcast(FP8X4),
-                    rhs_scale=scales,
-                    start=True,
-                    stop=True,
-                )
+                one_plane(bank[:, b, 0:count], e, 2 * u + b, codes, scales)
             return bank
 
         def empty(bank, u, first, count, results, on_vector=False):
@@ -138,26 +129,44 @@ def tile_moe_uni_none_kernel(
                 copy = nc.vector.tensor_copy if on_vector else nc.scalar.copy
                 copy(results[2 * u + b][:, first : first + count], bank[:, b, 0:count])
 
-        y = [keep.tile([P, S], F32, name="y%d" % j) for j in range(2)]
         for e in range(E):
             fetch_x_words(e)
         fetch_x_scales(0, "x_sc0")
-        late = []
+        fetch_x_scales(2, "x_sc2")
+        every = slice(0, 4)
+        early, late = [], []
         for e in range(E):
-            cast_w(e, 0)
-            cast_w(e, 1)
-            if e < E - 1:
-                quantize_w(e, (0, 1))
+            w_bf[e] = keep.tile([P, 4, P, 4], BF16, name="w_bf%d" % e, tag="w_bf%d" % e, align_bytes=64)
+            split = SCALAR_SHARE[e]
+            if e < LAST:
+                cast_w(nc.scalar.copy, e, w_raw[e], every, every, slice(0, split))
+                if split < P:
+                    cast_w(nc.vector.tensor_copy, e, w_raw[e], every, every, slice(split, P))
+                quantize_w(e, 0, 4)
+                early.append(multiply(e, 0, x_codes[e][:], x_sc[e], C))
+                if e < 2:
+                    late.append(multiply(e, 1, x_codes[e][:], x_sc[e], C))
             else:
-                quantize_w(e, (0,))
-                quantize_w(e, (1,))
-            if e == 0:
-                fetch_x_scales(2, "w_bf0")
-            bank = multiply(e, 0, x_codes[e][:], x_sc[e], C)
-            late.append(multiply(e, 1, x_codes[e][:], x_sc[e], C))
-            empty(bank, 0, e * C, C, y, e == E - 1)
-        y.extend(keep.tile([P, S], F32, name="y%d" % (2 + h), tag="w_bf%d" % (2 + h), align_bytes=64) for h in range(2))
+                cast_w(nc.scalar.copy, e, last_raw[0], slice(0, 2), every, slice(0, split))
+                cast_w(nc.vector.tensor_copy, e, last_raw[0], slice(0, 2), every, slice(split, P))
+                for b in range(2):
+                    cast_w(nc.vector.tensor_copy, e, last_raw[1], slice(2, 4), slice(b, b + 1), slice(0, P))
+                cast_w(nc.scalar.copy, e, last_raw[1], slice(2, 4), slice(2, 4), slice(0, P))
+                banks = [fw_psum.tile([P, C], F32, name="fw_bank") for b in range(2)]
+                for b in range(2):
+                    quantize_w(e, b, b + 1)
+                    one_plane(banks[b][:], e, b, x_codes[e][:], x_sc[e])
+        tenants = ("w_raw20", "w_bf2", "w_bf3", "w_raw32")
+        y = [keep.tile([P, S], F32, name="y%d" % j, tag=tenants[j], align_bytes=64) for j in range(4)]
+        for b in range(2):
+            for e in range(LAST):
+                nc.scalar.copy(y[b][:, e * C : (e + 1) * C], early[e][:, b, :])
+        nc.vector.tensor_copy(y[0][:, LAST * C : S], banks[0][:])
+        nc.scalar.copy(y[1][:, LAST * C : S], banks[1][:])
+        quantize_w(LAST, 2, 4)
         for e in range(E):
+            if e >= 2:
+                late.append(multiply(e, 1, x_codes[e][:], x_sc[e], C))
             empty(late[e], 1, e * C, C, y)
 
         gate_bank = fw_psum.tile([P, 2, 256], F32, name="fw_bank")
@@ -165,127 +174,153 @@ def tile_moe_uni_none_kernel(
         gate_cols = keep.tile([P, 16], F32, name="gate_cols")
         nc.scalar.copy(gate_cols[:], gate_bank[:, 0, 0:16])
 
-        def fetch_and_gate(step, results, lists, u, chunk):
-            bank = fw_psum.tile([P, 2, 256], F32, name="fw_bank")
+        def fetch_and_gate(step, results, lists, plane, first, count, between):
+            gated = keep.tile([P, 2, count], F32, name="gated%d%d_%d" % (step, plane, first))
             for r in range(2):
-                got = keep.tile([P, 2, P], F32, name="got%d%d%d%d" % (step, r, u, chunk))
-                for b in range(2):
-                    nc.vector.tensor_copy(got[:, b, :], results[2 * u + b][:].indirect(entries(lists[r], P * chunk, P)))
-                    nc.tensor.transpose(bank[:, r, P * b : P * (b + 1)], got[:, b, :], ident[:])
-            gated = keep.tile([P, 2, 256], F32, name="gated%d%d%d" % (step, u, chunk))
-            for r in range(2):
-                col = 8 * step + 4 * r + chunk
-                nc.scalar.activation(gated[:, r, :], bank[:, r, :], COPY, scale=gate_cols[:, col : col + 1])
+                name = "got%d%d%d_%d" % (step, r, plane, first)
+                got = keep.tile([P, count], F32, name=name, tag=name)
+                nc.vector.tensor_copy(got[:], results[plane][:].indirect(entries(lists[r], first, count)))
+                bank = fw_psum.tile([P, 4, P], F32, name="fw_bank")
+                for chunk in range(count // P):
+                    nc.tensor.transpose(bank[:, chunk, :], got[:, P * chunk : P * (chunk + 1)], ident[:])
+                if r == 1 and between is not None:
+                    between()
+                for chunk in range(count // P):
+                    col = 8 * step + 4 * r + first // P + chunk
+                    nc.scalar.activation(
+                        gated[:, r, P * chunk : P * (chunk + 1)],
+                        bank[:, chunk, :],
+                        COPY,
+                        scale=gate_cols[:, col : col + 1],
+                    )
             return gated
 
-        def turn_back(gated):
-            summed = acc_psum.tile([P, 2, 256], F32, name="acc_bank")
-            for b in range(2):
+        def turn_back(gated, chunks, dst):
+            for n, chunk in enumerate(chunks):
                 for r in range(2):
                     nc.tensor.matmul(
-                        summed[:, b, 0:P],
-                        gated[:, r, P * b : P * (b + 1)],
+                        dst[:, P * n : P * (n + 1)],
+                        gated[:, r, P * chunk : P * (chunk + 1)],
                         ident[:],
                         start=(r == 0),
                         stop=(r == 1),
                         is_transpose=True,
                     )
-            return summed[:, :, 0:P]
 
         def combine_turned(step, results, lists, units, finish):
-            waiting = None
-            for u, chunk in units:
-                gated = fetch_and_gate(step, results, lists, u, chunk)
-                if waiting is not None:
-                    finish(waiting[0], waiting[1], turn_back(waiting[2]))
-                waiting = (u, chunk, gated)
-            finish(waiting[0], waiting[1], turn_back(waiting[2]))
+            between, after = None, []
+            for n, (plane, first, count) in enumerate(units):
+                gated = fetch_and_gate(step, results, lists, plane, first, count, between)
+                for copy_out in after:
+                    copy_out("got%d1%d_%d" % (step, plane, first))
+                after = []
+                between = partial(finish, plane, first, count, gated, after)
+            between()
+            for copy_out in after:
+                copy_out("last")
 
-        def gated_products(step, results, lists, wide, u, first, count):
-            gates, gate_first = wide
-            prods = [keep.tile([P, 2, count], F32, name="prod%d%d%d_%d" % (step, r, u, first)) for r in range(2)]
-            for b in range(2):
-                for r in range(2):
-                    nc.vector.tensor_tensor(
-                        prods[r][:, b, :],
-                        results[2 * u + b][:].indirect(entries(lists[r], first, count)),
-                        gates[:, r, first - gate_first : first - gate_first + count],
-                        MULT,
-                    )
-            return prods
+        def gated_product(dst, window, lst, gates, first, count):
+            nc.vector.tensor_tensor(dst, window[:].indirect(entries(lst, first, count)), gates, MULT)
 
-        c_pairs = [keep.tile([P, T, 2], BF16, name="c_pairs%d" % u) for u in range(2)]
+        summed, rounded = {}, []
 
-        def round_c(u, chunk, summed):
-            nc.scalar.copy(c_pairs[u][:, P * chunk : P * (chunk + 1), :], summed.rearrange("p b t -> p t b"))
+        def round_c(plane, first, count, gated, after):
+            u, b = divmod(plane, 2)
+            for n in range(count // 256):
+                half = first // 256 + n
+                if b == 0:
+                    summed[half] = acc_psum.tile([P, 2, 256], F32, name="acc_bank")
+                turn_back(gated, (2 * n, 2 * n + 1), summed[half][:, b, :])
+                if b == 1:
+                    rounded.append((u, half, summed[half]))
 
-        combine_turned(0, y, (pos1_sb, pos2_sb), TURNED1, round_c)
-        for u, first, count in PLAIN1:
-            prods = gated_products(0, y, (pos1_sb, pos2_sb), wide1, u, first, count)
-            nc.vector.tensor_tensor(
-                c_pairs[u][:, first : first + count, :].rearrange("p (c i) b -> p c b i", i=4),
-                prods[0][:].rearrange("p b (c i) -> p c b i", i=4),
-                prods[1][:].rearrange("p b (c i) -> p c b i", i=4),
-                ADD,
-            )
+        combine_turned(0, y, (pos1_sb, pos2_sb), UNITS1, round_c)
+        c_pairs = [keep.tile([P, T, 2], BF16, name="c_pairs%d" % u, tag=("got013_0", "c_pairs1")[u]) for u in range(2)]
+        for u, half, bank in rounded:
+            nc.scalar.copy(c_pairs[u][:, 256 * half : 256 * (half + 1), :], bank[:].rearrange("p b t -> p t b"))
+        prods = [keep.tile([P, 2, 256], F32, name="prod0%d" % r) for r in range(2)]
+        for b in range(2):
+            for r, lst in enumerate((pos1_sb, pos2_sb)):
+                gated_product(prods[r][:, b, :], y[2 + b], lst, wide1[:, r, :], 256, 256)
+        nc.vector.tensor_tensor(
+            c_pairs[1][:, 256:T, :].rearrange("p (c i) b -> p c b i", i=4),
+            prods[0][:].rearrange("p b (c i) -> p c b i", i=4),
+            prods[1][:].rearrange("p b (c i) -> p c b i", i=4),
+            ADD,
+        )
         c_words = [c_pairs[u][:].rearrange("p t b -> p (t b)").bitcast(U32) for u in range(2)]
 
         z = [keep.tile([P, S], F32, name="z%d" % j) for j in range(2)]
         c_codes, c_sc, woven = {}, {}, {}
 
-        def fetch_slots(first, count, direct=False, tag=None):
+        def fetch_slots(first, count, tag, direct=False):
             name = "woven%d" % first
-            woven[first] = keep.tile([P, count, 2], U32, name=name, tag=(direct and tag) or name, align_bytes=64)
+            woven[first] = keep.tile([P, count, 2], U32, name=name, tag=tag if direct else name, align_bytes=64)
             if direct:
                 for u in range(2):
                     nc.vector.tensor_copy(woven[first][:, :, u], c_words[u].indirect(entries(offs2_sb, first, count)))
             else:
-                name = "pairs%d" % first
-                pairs = keep.tile([P, 2, count], U32, name=name, tag=tag or name, align_bytes=64)
+                pairs = keep.tile([P, 2, count], U32, name="pairs%d" % first, tag=tag, align_bytes=64)
                 for u in range(2):
                     nc.vector.tensor_copy(pairs[:, u, :], c_words[u].indirect(entries(offs2_sb, first, count)))
                 nc.scalar.copy(woven[first][:].bitcast(F32), pairs[:].bitcast(F32).rearrange("p u s -> p s u"))
 
-        def quantize_slots(first, count, on_vector=False):
-            c_codes[first] = keep.tile([P, count], U32, name="c_codes%d" % first, align_bytes=64)
+        def quantize_slots(first, count, tag=None):
+            name = "c_codes%d" % first
+            c_codes[first] = keep.tile([P, count], U32, name=name, tag=tag or name, align_bytes=64)
             c_sc[first] = keep.tile([P, count], U8, name="c_sc%d" % first, align_bytes=64)
             nc.vector.quantize_mx(
                 c_codes[first][:].bitcast(FP8X4),
                 c_sc[first][:],
                 woven[first][:].rearrange("p s u -> p (s u)").bitcast(BF16),
             )
-            bank = multiply(first // C, 0, c_codes[first][:], c_sc[first][:], count)
-            empty(bank, 0, first, count, z, on_vector)
+            if first < LAST * C:
+                bank = multiply(first // C, 0, c_codes[first][:], c_sc[first][:], count)
+                empty(bank, 0, first, count, z)
+            else:
+                for b in range(2):
+                    dst = banks[b][:, first - LAST * C : first - LAST * C + count]
+                    one_plane(dst, LAST, b, c_codes[first][:], c_sc[first][:])
 
-        fetch_slots(0, 256)
-        fetch_slots(256, 256)
+        fetch_slots(0, 256, "pairs0")
+        fetch_slots(256, 256, "pairs256")
+        fetch_slots(512, 256, "pairs512")
         quantize_slots(0, 256)
-        fetch_slots(512, 256, False, "woven0")
         quantize_slots(256, 256)
-        fetch_slots(768, P, False, "woven256")
+        fetch_slots(768, P, "pairs256", True)
         quantize_slots(512, 256)
-        fetch_slots(896, P, True, "woven512")
-        quantize_slots(768, P, True)
-        quantize_slots(896, P, True)
-        z.append(keep.tile([P, S], F32, name="z2", tag="woven768", align_bytes=64))
-        z.append(keep.tile([P, S], F32, name="z3", tag="woven512", align_bytes=64))
+        fetch_slots(896, P, "pairs512", True)
+        banks = [fw_psum.tile([P, C], F32, name="fw_bank") for b in range(2)]
+        quantize_slots(768, P, "woven512")
+        quantize_slots(896, P)
+        nc.vector.tensor_copy(z[0][:, LAST * C : S], banks[0][:])
+        nc.scalar.copy(z[1][:, LAST * C : S], banks[1][:])
+        z.append(keep.tile([P, S], F32, name="z2", tag="pairs512", align_bytes=64))
+        z.append(keep.tile([P, S], F32, name="z3", tag="pairs256", align_bytes=64))
         for first, count in ((0, 256), (256, 256), (512, 256), (768, P), (896, P)):
             bank = multiply(first // C, 1, c_codes[first][:], c_sc[first][:], count)
             empty(bank, 1, first, count, z)
 
         out_planes = out.rearrange("(p j) t -> p j t", j=4)
-        staged = [keep.tile([P, 2, T], F32, name="staged%d" % u) for u in range(2)]
 
-        def store(u, chunk, summed):
-            nc.scalar.copy(staged[u][:, :, P * chunk : P * (chunk + 1)], summed)
-            if chunk % 2 == 1 or (u, chunk) == TURNED2[-1]:
-                tokens = slice(P * (chunk - chunk % 2), P * (chunk + 1))
-                nc.scalar.dma_start(out_planes[:, 2 * u : 2 * u + 2, tokens], staged[u][:, :, tokens])
+        def copy_and_store(plane, src, first, count, tag):
+            staged = keep.tile([P, count], F32, name="staged%d_%d" % (plane, first), tag=tag)
+            nc.scalar.copy(staged[:], src[:, 0:count])
+            nc.scalar.dma_start(out_planes[:, plane, first : first + count], staged[:])
 
-        combine_turned(1, z, (pos3_sb, pos4_sb), TURNED2, store)
-        for u, first, count in PLAIN2:
-            prods = gated_products(1, z, (pos3_sb, pos4_sb), wide2, u, first, count)
-            for b in range(2):
-                total = keep.tile([P, count], F32, name="total%d%d_%d" % (u, b, first))
-                nc.vector.tensor_tensor(total[:], prods[0][:, b, :], prods[1][:, b, :], ADD)
-                nc.sync.dma_start(out_planes[:, 2 * u + b, first : first + count], total[:])
+        def store(plane, first, count, gated, after):
+            bank = acc_psum.tile([P, 2, 256], F32, name="acc_bank")
+            flat = bank[:].rearrange("p b t -> p (b t)")
+            turn_back(gated, range(count // P), flat)
+            after.append(partial(copy_and_store, plane, flat, first, count))
+
+        combine_turned(1, z, (pos3_sb, pos4_sb), UNITS2, store)
+        prod3 = keep.tile([P, T], F32, name="prod3")
+        gated_product(prod3[:], z[3], pos3_sb, wide2[:, 0, :], 0, T)
+        prod4 = keep.tile([P, T], F32, name="prod4")
+        for first in (0, 256):
+            gated_product(prod4[:, first : first + 256], z[3], pos4_sb, wide2[:, 1, first : first + 256], first, 256)
+        for first in (0, 256):
+            total = keep.tile([P, 256], F32, name="total%d" % first)
+            nc.vector.tensor_tensor(total[:], prod3[:, first : first + 256], prod4[:, first : first + 256], ADD)
+            nc.sync.dma_start(out_planes[:, 3, first : first + 256], total[:])

@@ -21,8 +21,10 @@ ADD = mybir.AluOpType.add
 COPY = mybir.ActivationFunctionType.Copy
 
 LAST = E - 1
-UNITS1 = ((0,0,256),(0,256,256),(1,0,512),(2,0,256),(3,0,256))
-UNITS2 = ((0,0,256),(0,256,256),(1,0,256),(1,256,256),(2,0,256),(2,256,256))
+UNITS1 = ((0,0,256),(0,256,256),(1,0,512),(2,0,384),(3,0,384))
+UNITS2 = ((0,0,256),(0,256,256),(1,0,256),(1,256,256),(2,0,256),(2,256,256),(3,0,256))
+PLAIN1 = 384
+PLAIN2 = 256
 SCALAR_SHARE = (128, 64, 48, 64)
 
 
@@ -75,11 +77,11 @@ def tile_moe_uni_none_kernel(
         for n, gate in enumerate((gate1, gate2)):
             rows = gate.rearrange("r p (c n) -> (r p c) n", n=P)
             nc.sync.dma_start(gate_rows[8 * n : 8 * n + 8, :], rows[508:516, :])
-        wide1 = load_wide(gate1, 256, "wide1")
+        wide1 = load_wide(gate1, PLAIN1, "wide1")
         offs2_sb = load_list(offs2, "offs2_sb")
         pos3_sb = load_list(pos3, "pos3_sb")
         pos4_sb = load_list(pos4, "pos4_sb")
-        wide2 = load_wide(gate2, 0, "wide2")
+        wide2 = load_wide(gate2, PLAIN2, "wide2")
 
         x_codes, x_sc, w_bf, w_codes, w_sc = {}, {}, {}, {}, {}
 
@@ -124,6 +126,21 @@ def tile_moe_uni_none_kernel(
                 one_plane(bank[:, b, 0:count], e, 2 * u + b, codes, scales)
             return bank
 
+        def late_banks(half, pieces):
+            made = []
+            for plane in (2, 3):
+                bank = acc_psum.tile([P, 512], F32, name="acc_bank")
+                for first, count, codes, scales in pieces:
+                    if first // 512 == half:
+                        one_plane(bank[:, first % 512 : first % 512 + count], first // C, plane, codes, scales)
+                made.append(bank)
+            return made
+
+        def empty_late(step, results, late, plane, tag):
+            results.append(keep.tile([P, S], F32, name="late%d%d" % (step, plane), tag=tag, align_bytes=64))
+            for half in range(2):
+                nc.scalar.copy(results[plane][:, 512 * half : 512 * (half + 1)], late[half][plane - 2][:])
+
         def empty(bank, u, first, count, results, on_vector=False):
             for b in range(2):
                 copy = nc.vector.tensor_copy if on_vector else nc.scalar.copy
@@ -134,7 +151,8 @@ def tile_moe_uni_none_kernel(
         fetch_x_scales(0, "x_sc0")
         fetch_x_scales(2, "x_sc2")
         every = slice(0, 4)
-        early, late = [], []
+        early = []
+        tokens1 = [(e * C, C, x_codes[e][:], x_sc[e]) for e in range(E)]
         for e in range(E):
             w_bf[e] = keep.tile([P, 4, P, 4], BF16, name="w_bf%d" % e, tag="w_bf%d" % e, align_bytes=64)
             split = SCALAR_SHARE[e]
@@ -144,8 +162,8 @@ def tile_moe_uni_none_kernel(
                     cast_w(nc.vector.tensor_copy, e, w_raw[e], every, every, slice(split, P))
                 quantize_w(e, 0, 4)
                 early.append(multiply(e, 0, x_codes[e][:], x_sc[e], C))
-                if e < 2:
-                    late.append(multiply(e, 1, x_codes[e][:], x_sc[e], C))
+                if e == 1:
+                    late = late_banks(0, tokens1)
             else:
                 cast_w(nc.scalar.copy, e, last_raw[0], slice(0, 2), every, slice(0, split))
                 cast_w(nc.vector.tensor_copy, e, last_raw[0], slice(0, 2), every, slice(split, P))
@@ -156,29 +174,26 @@ def tile_moe_uni_none_kernel(
                 for b in range(2):
                     quantize_w(e, b, b + 1)
                     one_plane(banks[b][:], e, b, x_codes[e][:], x_sc[e])
-        tenants = ("w_raw20", "w_bf2", "w_bf3", "w_raw32")
-        y = [keep.tile([P, S], F32, name="y%d" % j, tag=tenants[j], align_bytes=64) for j in range(4)]
+        gate_bank = fw_psum.tile([P, 2, 256], F32, name="fw_bank")
+        nc.tensor.transpose(gate_bank[:, 0, 0:P], gate_rows[:], ident[:])
+        gate_cols = keep.tile([P, 16], F32, name="gate_cols")
+        nc.scalar.copy(gate_cols[:], gate_bank[:, 0, 0:16])
+
+        tenants = ("w_raw20", "w_bf2")
+        y = [keep.tile([P, S], F32, name="y%d" % j, tag=tenants[j], align_bytes=64) for j in range(2)]
         for b in range(2):
             for e in range(LAST):
                 nc.scalar.copy(y[b][:, e * C : (e + 1) * C], early[e][:, b, :])
         nc.vector.tensor_copy(y[0][:, LAST * C : S], banks[0][:])
         nc.scalar.copy(y[1][:, LAST * C : S], banks[1][:])
         quantize_w(LAST, 2, 4)
-        for e in range(E):
-            if e >= 2:
-                late.append(multiply(e, 1, x_codes[e][:], x_sc[e], C))
-            empty(late[e], 1, e * C, C, y)
-
-        gate_bank = fw_psum.tile([P, 2, 256], F32, name="fw_bank")
-        nc.tensor.transpose(gate_bank[:, 0, 0:P], gate_rows[:], ident[:])
-        gate_cols = keep.tile([P, 16], F32, name="gate_cols")
-        nc.scalar.copy(gate_cols[:], gate_bank[:, 0, 0:16])
+        late = [late, late_banks(1, tokens1)]
 
         def fetch_and_gate(step, results, lists, plane, first, count, between):
             gated = keep.tile([P, 2, count], F32, name="gated%d%d_%d" % (step, plane, first))
             for r in range(2):
                 name = "got%d%d%d_%d" % (step, r, plane, first)
-                got = keep.tile([P, count], F32, name=name, tag=name)
+                got = keep.tile([P, count], F32, name=name, tag=name, align_bytes=64)
                 nc.vector.tensor_copy(got[:], results[plane][:].indirect(entries(lists[r], first, count)))
                 bank = fw_psum.tile([P, 4, P], F32, name="fw_bank")
                 for chunk in range(count // P):
@@ -207,43 +222,49 @@ def tile_moe_uni_none_kernel(
                         is_transpose=True,
                     )
 
-        def combine_turned(step, results, lists, units, finish):
+        def combine_turned(step, results, lists, units, finish, late):
             between, after = None, []
+            empty_late(step, results, late, 2, ("w_bf3", "pairs512")[step])
             for n, (plane, first, count) in enumerate(units):
                 gated = fetch_and_gate(step, results, lists, plane, first, count, between)
+                if n == 1:
+                    empty_late(step, results, late, 3, "got%d0%d_%d" % (step, plane, first))
                 for copy_out in after:
                     copy_out("got%d1%d_%d" % (step, plane, first))
                 after = []
                 between = partial(finish, plane, first, count, gated, after)
             between()
             for copy_out in after:
-                copy_out("last")
+                copy_out("last%d" % step)
 
         def gated_product(dst, window, lst, gates, first, count):
             nc.vector.tensor_tensor(dst, window[:].indirect(entries(lst, first, count)), gates, MULT)
 
-        summed, rounded = {}, []
+        summed, c_pairs = {}, {}
 
-        def round_c(plane, first, count, gated, after):
+        def round_c(u, first, count, bank, tag):
+            if u not in c_pairs:
+                c_pairs[u] = keep.tile([P, T, 2], BF16, name="c_pairs%d" % u, tag=tag, align_bytes=64)
+            nc.scalar.copy(c_pairs[u][:, first : first + count, :], bank[:, :, 0:count].rearrange("p b t -> p t b"))
+
+        def sum_c(plane, first, count, gated, after):
             u, b = divmod(plane, 2)
-            for n in range(count // 256):
-                half = first // 256 + n
+            for at in range(0, count, 256):
+                width = min(256, count - at)
                 if b == 0:
-                    summed[half] = acc_psum.tile([P, 2, 256], F32, name="acc_bank")
-                turn_back(gated, (2 * n, 2 * n + 1), summed[half][:, b, :])
+                    summed[first + at] = acc_psum.tile([P, 2, 256], F32, name="acc_bank")
+                turn_back(gated, range(at // P, (at + width) // P), summed[first + at][:, b, :])
                 if b == 1:
-                    rounded.append((u, half, summed[half]))
+                    after.append(partial(round_c, u, first + at, width, summed[first + at]))
 
-        combine_turned(0, y, (pos1_sb, pos2_sb), UNITS1, round_c)
-        c_pairs = [keep.tile([P, T, 2], BF16, name="c_pairs%d" % u, tag=("got013_0", "c_pairs1")[u]) for u in range(2)]
-        for u, half, bank in rounded:
-            nc.scalar.copy(c_pairs[u][:, 256 * half : 256 * (half + 1), :], bank[:].rearrange("p b t -> p t b"))
-        prods = [keep.tile([P, 2, 256], F32, name="prod0%d" % r) for r in range(2)]
+        combine_turned(0, y, (pos1_sb, pos2_sb), UNITS1, sum_c, late)
+        count = T - PLAIN1
+        prods = [keep.tile([P, 2, count], F32, name="prod0%d" % r) for r in range(2)]
         for b in range(2):
             for r, lst in enumerate((pos1_sb, pos2_sb)):
-                gated_product(prods[r][:, b, :], y[2 + b], lst, wide1[:, r, :], 256, 256)
+                gated_product(prods[r][:, b, :], y[2 + b], lst, wide1[:, r, :], PLAIN1, count)
         nc.vector.tensor_tensor(
-            c_pairs[1][:, 256:T, :].rearrange("p (c i) b -> p c b i", i=4),
+            c_pairs[1][:, PLAIN1:T, :].rearrange("p (c i) b -> p c b i", i=4),
             prods[0][:].rearrange("p b (c i) -> p c b i", i=4),
             prods[1][:].rearrange("p b (c i) -> p c b i", i=4),
             ADD,
@@ -251,19 +272,23 @@ def tile_moe_uni_none_kernel(
         c_words = [c_pairs[u][:].rearrange("p t b -> p (t b)").bitcast(U32) for u in range(2)]
 
         z = [keep.tile([P, S], F32, name="z%d" % j) for j in range(2)]
-        c_codes, c_sc, woven = {}, {}, {}
+        c_codes, c_sc, woven, pairs = {}, {}, {}, {}
 
-        def fetch_slots(first, count, tag, direct=False):
+        def fetch_pairs(first, count, u):
+            if u == 0:
+                name = "pairs%d" % first
+                pairs[first] = keep.tile([P, 2, count], U32, name=name, tag=name, align_bytes=64)
+            nc.vector.tensor_copy(pairs[first][:, u, :], c_words[u].indirect(entries(offs2_sb, first, count)))
+
+        def weave(first, count):
             name = "woven%d" % first
-            woven[first] = keep.tile([P, count, 2], U32, name=name, tag=tag if direct else name, align_bytes=64)
-            if direct:
-                for u in range(2):
-                    nc.vector.tensor_copy(woven[first][:, :, u], c_words[u].indirect(entries(offs2_sb, first, count)))
-            else:
-                pairs = keep.tile([P, 2, count], U32, name="pairs%d" % first, tag=tag, align_bytes=64)
-                for u in range(2):
-                    nc.vector.tensor_copy(pairs[:, u, :], c_words[u].indirect(entries(offs2_sb, first, count)))
-                nc.scalar.copy(woven[first][:].bitcast(F32), pairs[:].bitcast(F32).rearrange("p u s -> p s u"))
+            woven[first] = keep.tile([P, count, 2], U32, name=name, tag=name, align_bytes=64)
+            nc.scalar.copy(woven[first][:].bitcast(F32), pairs[first][:].bitcast(F32).rearrange("p u s -> p s u"))
+
+        def fetch_woven(first, count, u, tag):
+            if first not in woven:
+                woven[first] = keep.tile([P, count, 2], U32, name="woven%d" % first, tag=tag, align_bytes=64)
+            nc.vector.tensor_copy(woven[first][:, :, u], c_words[u].indirect(entries(offs2_sb, first, count)))
 
         def quantize_slots(first, count, tag=None):
             name = "c_codes%d" % first
@@ -282,29 +307,30 @@ def tile_moe_uni_none_kernel(
                     dst = banks[b][:, first - LAST * C : first - LAST * C + count]
                     one_plane(dst, LAST, b, c_codes[first][:], c_sc[first][:])
 
-        fetch_slots(0, 256, "pairs0")
-        fetch_slots(256, 256, "pairs256")
-        fetch_slots(512, 256, "pairs512")
+        for first in (0, 256, 512):
+            fetch_pairs(first, 256, 0)
+        for first in (0, 256, 512):
+            fetch_pairs(first, 256, 1)
+            weave(first, 256)
         quantize_slots(0, 256)
         quantize_slots(256, 256)
-        fetch_slots(768, P, "pairs256", True)
+        for u in range(2):
+            fetch_woven(768, P, u, "pairs256")
         quantize_slots(512, 256)
-        fetch_slots(896, P, "pairs512", True)
+        for u in range(2):
+            fetch_woven(896, P, u, "pairs512")
         banks = [fw_psum.tile([P, C], F32, name="fw_bank") for b in range(2)]
         quantize_slots(768, P, "woven512")
         quantize_slots(896, P)
         nc.vector.tensor_copy(z[0][:, LAST * C : S], banks[0][:])
         nc.scalar.copy(z[1][:, LAST * C : S], banks[1][:])
-        z.append(keep.tile([P, S], F32, name="z2", tag="pairs512", align_bytes=64))
-        z.append(keep.tile([P, S], F32, name="z3", tag="pairs256", align_bytes=64))
-        for first, count in ((0, 256), (256, 256), (512, 256), (768, P), (896, P)):
-            bank = multiply(first // C, 1, c_codes[first][:], c_sc[first][:], count)
-            empty(bank, 1, first, count, z)
+        tokens2 = [(first, count, c_codes[first][:], c_sc[first][:]) for first, count in ((0, 256), (256, 256), (512, 256), (768, P), (896, P))]
+        late = [late_banks(half, tokens2) for half in range(2)]
 
         out_planes = out.rearrange("(p j) t -> p j t", j=4)
 
         def copy_and_store(plane, src, first, count, tag):
-            staged = keep.tile([P, count], F32, name="staged%d_%d" % (plane, first), tag=tag)
+            staged = keep.tile([P, count], F32, name="staged%d_%d" % (plane, first), tag=tag, align_bytes=64)
             nc.scalar.copy(staged[:], src[:, 0:count])
             nc.scalar.dma_start(out_planes[:, plane, first : first + count], staged[:])
 
@@ -314,13 +340,15 @@ def tile_moe_uni_none_kernel(
             turn_back(gated, range(count // P), flat)
             after.append(partial(copy_and_store, plane, flat, first, count))
 
-        combine_turned(1, z, (pos3_sb, pos4_sb), UNITS2, store)
-        prod3 = keep.tile([P, T], F32, name="prod3")
-        gated_product(prod3[:], z[3], pos3_sb, wide2[:, 0, :], 0, T)
-        prod4 = keep.tile([P, T], F32, name="prod4")
-        for first in (0, 256):
-            gated_product(prod4[:, first : first + 256], z[3], pos4_sb, wide2[:, 1, first : first + 256], first, 256)
-        for first in (0, 256):
-            total = keep.tile([P, 256], F32, name="total%d" % first)
-            nc.vector.tensor_tensor(total[:], prod3[:, first : first + 256], prod4[:, first : first + 256], ADD)
-            nc.sync.dma_start(out_planes[:, 3, first : first + 256], total[:])
+        combine_turned(1, z, (pos3_sb, pos4_sb), UNITS2, store, late)
+        count = T - PLAIN2
+        prod3 = keep.tile([P, count], F32, name="prod3")
+        gated_product(prod3[:], z[3], pos3_sb, wide2[:, 0, :], PLAIN2, count)
+        prod4 = keep.tile([P, count], F32, name="prod4")
+        halves = [slice(0, count // 2), slice(count // 2, count)]
+        for half in halves:
+            gated_product(prod4[:, half], z[3], pos4_sb, wide2[:, 1, half], PLAIN2 + half.start, count // 2)
+        for half in halves:
+            total = keep.tile([P, count // 2], F32, name="total%d" % half.start)
+            nc.vector.tensor_tensor(total[:], prod3[:, half], prod4[:, half], ADD)
+            nc.sync.dma_start(out_planes[:, 3, PLAIN2 + half.start : PLAIN2 + half.stop], total[:])

@@ -21,10 +21,10 @@ ADD = mybir.AluOpType.add
 COPY = mybir.ActivationFunctionType.Copy
 
 LAST = E - 1
-UNITS1 = ((0,0,256),(0,256,256),(1,0,512),(2,0,384),(3,0,384))
-UNITS2 = ((0,0,256),(0,256,256),(1,0,256),(1,256,256),(2,0,256),(2,256,256),(3,0,256))
-PLAIN1 = 384
-PLAIN2 = 256
+UNITS1 = ((0,0,256),(0,256,256),(1,0,512),(2,0,256),(3,0,256))
+UNITS2 = ((0,0,256),(0,256,256),(1,0,256),(1,256,256),(2,0,256),(2,256,256))
+PLAIN1 = 256
+PLAIN2 = 0
 SCALAR_SHARE = (128, 64, 48, 64)
 
 
@@ -190,7 +190,8 @@ def tile_moe_uni_none_kernel(
         late = [late, late_banks(1, tokens1)]
 
         def fetch_and_gate(step, results, lists, plane, first, count, between):
-            gated = keep.tile([P, 2, count], F32, name="gated%d%d_%d" % (step, plane, first))
+            name = "gated%d%d_%d" % (step, plane, first)
+            gated = keep.tile([P, 2, count], F32, name=name, tag=name, align_bytes=64)
             for r in range(2):
                 name = "got%d%d%d_%d" % (step, r, plane, first)
                 got = keep.tile([P, count], F32, name=name, tag=name, align_bytes=64)
@@ -235,7 +236,7 @@ def tile_moe_uni_none_kernel(
                 between = partial(finish, plane, first, count, gated, after)
             between()
             for copy_out in after:
-                copy_out("last%d" % step)
+                copy_out("gated%d%d_%d" % (step, plane, first))
 
         def gated_product(dst, window, lst, gates, first, count):
             nc.vector.tensor_tensor(dst, window[:].indirect(entries(lst, first, count)), gates, MULT)
@@ -262,7 +263,9 @@ def tile_moe_uni_none_kernel(
         prods = [keep.tile([P, 2, count], F32, name="prod0%d" % r) for r in range(2)]
         for b in range(2):
             for r, lst in enumerate((pos1_sb, pos2_sb)):
-                gated_product(prods[r][:, b, :], y[2 + b], lst, wide1[:, r, :], PLAIN1, count)
+                got = keep.tile([P, count], F32, name="plain%d%d" % (r, b))
+                nc.vector.tensor_copy(got[:], y[2 + b][:].indirect(entries(lst, PLAIN1, count)))
+                nc.gpsimd.tensor_tensor(prods[r][:, b, :], got[:], wide1[:, r, :], MULT)
         nc.vector.tensor_tensor(
             c_pairs[1][:, PLAIN1:T, :].rearrange("p (c i) b -> p c b i", i=4),
             prods[0][:].rearrange("p b (c i) -> p c b i", i=4),
@@ -309,18 +312,19 @@ def tile_moe_uni_none_kernel(
 
         for first in (0, 256, 512):
             fetch_pairs(first, 256, 0)
+        fetch_pairs(768, P, 0)
         for first in (0, 256, 512):
             fetch_pairs(first, 256, 1)
             weave(first, 256)
+        fetch_pairs(768, P, 1)
+        weave(768, P)
         quantize_slots(0, 256)
         quantize_slots(256, 256)
-        for u in range(2):
-            fetch_woven(768, P, u, "pairs256")
         quantize_slots(512, 256)
         for u in range(2):
             fetch_woven(896, P, u, "pairs512")
         banks = [fw_psum.tile([P, C], F32, name="fw_bank") for b in range(2)]
-        quantize_slots(768, P, "woven512")
+        quantize_slots(768, P)
         quantize_slots(896, P)
         nc.vector.tensor_copy(z[0][:, LAST * C : S], banks[0][:])
         nc.scalar.copy(z[1][:, LAST * C : S], banks[1][:])

from contextlib import ExitStack
from functools import partial

import concourse.mybir as mybir
from concourse.masks import make_identity

K, T, E, C = 512, 512, 4, 256
S = E * C
P = 128
FLOPS = 2 * 2 * K * K * S

F32 = mybir.dt.float32
BF16 = mybir.dt.bfloat16
I32 = mybir.dt.int32
U32 = mybir.dt.uint32
U16 = mybir.dt.uint16
U8 = mybir.dt.uint8
FP8X4 = mybir.dt.float8_e4m3fn_x4
MULT = mybir.AluOpType.mult
ADD = mybir.AluOpType.add
COPY = mybir.ActivationFunctionType.Copy

LAST = E - 1
UNITS1 = ((0,0,256),(0,256,256),(1,0,512),(2,0,256),(3,0,256))
UNITS2 = ((0,0,256),(0,256,256),(1,0,256),(1,256,256),(2,0,256),(2,256,256))
PLAIN1 = 256
PLAIN2 = 0
SCALAR_SHARE = (128, 64, 48, 64)


def entries(lst, first, count):
    return lst[:, first // 16 : (first + count) // 16]


def tile_moe_uni_none_kernel(
    tc, x_words, x_scales, w, gate1, gate2, offs, pos1, pos2, offs2, pos3, pos4, out
):
    nc = tc.nc
    with ExitStack() as ctx:
        keep = ctx.enter_context(tc.tile_pool(name="keep", bufs=1))
        fw_psum = ctx.enter_context(tc.psum_pool(name="fw_psum", bufs=3))
        acc_psum = ctx.enter_context(tc.psum_pool(name="acc_psum", bufs=5))

        def load_list(src, name):
            t = keep.tile(list(src.shape), U16, name=name)
            nc.sync.dma_start(t[:], src)
            return t

        def load_w(e, rows):
            name = "w_raw%d%d" % (e, rows[0])
            raw = keep.tile([P, len(rows), K], F32, name=name, tag=name, align_bytes=64)
            nc.sync.dma_start(raw[:], w[e].rearrange("(p j) n -> p j n", j=4)[:, rows[0] : rows[-1] + 1, :])
            return raw

        def load_wide(gate, first, name):
            wide = keep.tile([P, 2, T - first], F32, name=name)
            nc.sync.dma_start(wide[:], gate.rearrange("r p t -> p r t")[:, :, first:T])
            return wide

        x_planes = keep.tile([P, T], U8, name="x_planes", align_bytes=64)
        nc.vector.memset(x_planes[:].bitcast(I32), 0)
        ident = keep.tile([P, P], F32, name="ident")
        make_identity(nc, ident[:])
        gate_rows = keep.tile([P, P], F32, name="gate_rows")
        nc.scalar.activation(gate_rows[:], ident[:], COPY, scale=0.0)

        offs_sb = load_list(offs, "offs_sb")
        x_sb = keep.tile([P, T], I32, name="x_sb", align_bytes=64)
        nc.sync.dma_start(x_sb[:], x_words[0].rearrange("p t d -> p (t d)").bitcast(I32))
        pos1_sb = load_list(pos1, "pos1_sb")
        scale_rows = x_scales[0].rearrange("(q r) t -> r q t", r=4)
        for r in range(4):
            nc.sync.dma_start(x_planes[r:P:32, :].bitcast(I32), scale_rows[r].bitcast(I32))
        w_raw = [load_w(e, range(4)) for e in range(LAST)]
        last_raw = [load_w(LAST, range(2)), load_w(LAST, range(2, 4))]
        pos2_sb = load_list(pos2, "pos2_sb")
        for n, gate in enumerate((gate1, gate2)):
            rows = gate.rearrange("r p (c n) -> (r p c) n", n=P)
            nc.sync.dma_start(gate_rows[8 * n : 8 * n + 8, :], rows[508:516, :])
        wide1 = load_wide(gate1, PLAIN1, "wide1")
        offs2_sb = load_list(offs2, "offs2_sb")
        pos3_sb = load_list(pos3, "pos3_sb")
        pos4_sb = load_list(pos4, "pos4_sb")
        wide2 = load_wide(gate2, PLAIN2, "wide2")

        x_codes, x_sc, w_bf, w_codes, w_sc = {}, {}, {}, {}, {}

        def fetch_x_words(e):
            x_codes[e] = keep.tile([P, C], U32, name="x_codes%d" % e, align_bytes=64)
            nc.vector.tensor_copy(x_codes[e][:], x_sb[:].bitcast(U32).indirect(entries(offs_sb, e * C, C)))

        def fetch_x_scales(first_e, tag):
            both = keep.tile([P, 2, C], U8, name="x_sc%d" % first_e, tag=tag, align_bytes=64)
            for n in range(2):
                x_sc[first_e + n] = both[:, n, :]
                nc.vector.tensor_copy(both[:, n, :], x_planes[:].indirect(entries(offs_sb, (first_e + n) * C, C)))

        def cast_w(copy, e, raw, rows, planes, ms):
            dst = w_bf[e][:, planes, ms, rows].rearrange("p t m j -> p m j t")
            src = raw[:].rearrange("p j (m t) -> p m j t", t=4)[:, ms, :, planes]
            copy(dst, src)

        def quantize_w(e, first, last):
            if first == 0:
                w_codes[e] = keep.tile([P, K], U32, name="w_codes%d" % e, align_bytes=64)
                w_sc[e] = keep.tile([P, K], U8, name="w_sc%d" % e, align_bytes=64)
            cols = slice(P * first, P * last)
            src = w_bf[e][:, first:last, :, :].rearrange("p t m j -> p (t m j)")
            nc.vector.quantize_mx(w_codes[e][:, cols].bitcast(FP8X4), w_sc[e][:, cols], src)

        def one_plane(dst, e, plane, codes, scales):
            cols = slice(P * plane, P * (plane + 1))
            nc.tensor.matmul_mx(
                out=dst,
                lhsT=w_codes[e][:, cols].bitcast(FP8X4),
                lhsT_scale=w_sc[e][:, cols],
                rhs=codes.bitcast(FP8X4),
                rhs_scale=scales,
                start=True,
                stop=True,
            )

        def multiply(e, u, codes, scales, count):
            bank = acc_psum.tile([P, 2, 256], F32, name="acc_bank")
            for b in range(2):
                one_plane(bank[:, b, 0:count], e, 2 * u + b, codes, scales)
            return bank

        def late_banks(half, pieces):
            made = []
            for plane in (2, 3):
                bank = acc_psum.tile([P, 512], F32, name="acc_bank")
                for first, count, codes, scales in pieces:
                    if first // 512 == half:
                        one_plane(bank[:, first % 512 : first % 512 + count], first // C, plane, codes, scales)
                made.append(bank)
            return made

        def empty_late(step, results, late, plane, tag):
            results.append(keep.tile([P, S], F32, name="late%d%d" % (step, plane), tag=tag, align_bytes=64))
            for half in range(2):
                nc.scalar.copy(results[plane][:, 512 * half : 512 * (half + 1)], late[half][plane - 2][:])

        def empty(bank, u, first, count, results, on_vector=False):
            for b in range(2):
                copy = nc.vector.tensor_copy if on_vector else nc.scalar.copy
                copy(results[2 * u + b][:, first : first + count], bank[:, b, 0:count])

        for e in range(E):
            fetch_x_words(e)
        fetch_x_scales(0, "x_sc0")
        fetch_x_scales(2, "x_sc2")
        every = slice(0, 4)
        early = []
        tokens1 = [(e * C, C, x_codes[e][:], x_sc[e]) for e in range(E)]
        for e in range(E):
            w_bf[e] = keep.tile([P, 4, P, 4], BF16, name="w_bf%d" % e, tag="w_bf%d" % e, align_bytes=64)
            split = SCALAR_SHARE[e]
            if e < LAST:
                cast_w(nc.scalar.copy, e, w_raw[e], every, every, slice(0, split))
                if split < P:
                    cast_w(nc.vector.tensor_copy, e, w_raw[e], every, every, slice(split, P))
                quantize_w(e, 0, 4)
                early.append(multiply(e, 0, x_codes[e][:], x_sc[e], C))
                if e == 1:
                    late = late_banks(0, tokens1)
            else:
                cast_w(nc.scalar.copy, e, last_raw[0], slice(0, 2), every, slice(0, split))
                cast_w(nc.vector.tensor_copy, e, last_raw[0], slice(0, 2), every, slice(split, P))
                for b in range(2):
                    cast_w(nc.vector.tensor_copy, e, last_raw[1], slice(2, 4), slice(b, b + 1), slice(0, P))
                cast_w(nc.scalar.copy, e, last_raw[1], slice(2, 4), slice(2, 4), slice(0, P))
                banks = [fw_psum.tile([P, C], F32, name="fw_bank") for b in range(2)]
                for b in range(2):
                    quantize_w(e, b, b + 1)
                    one_plane(banks[b][:], e, b, x_codes[e][:], x_sc[e])
        gate_bank = fw_psum.tile([P, 2, 256], F32, name="fw_bank")
        nc.tensor.transpose(gate_bank[:, 0, 0:P], gate_rows[:], ident[:])
        gate_cols = keep.tile([P, 16], F32, name="gate_cols")
        nc.scalar.copy(gate_cols[:], gate_bank[:, 0, 0:16])

        tenants = ("w_raw20", "w_bf2")
        y = [keep.tile([P, S], F32, name="y%d" % j, tag=tenants[j], align_bytes=64) for j in range(2)]
        for b in range(2):
            for e in range(LAST):
                nc.scalar.copy(y[b][:, e * C : (e + 1) * C], early[e][:, b, :])
        nc.vector.tensor_copy(y[0][:, LAST * C : S], banks[0][:])
        nc.scalar.copy(y[1][:, LAST * C : S], banks[1][:])
        quantize_w(LAST, 2, 4)
        late = [late, late_banks(1, tokens1)]

        def fetch_and_gate(step, results, lists, plane, first, count, between):
            name = "gated%d%d_%d" % (step, plane, first)
            gated = keep.tile([P, 2, count], F32, name=name, tag=name, align_bytes=64)
            for r in range(2):
                name = "got%d%d%d_%d" % (step, r, plane, first)
                got = keep.tile([P, count], F32, name=name, tag=name, align_bytes=64)
                nc.vector.tensor_copy(got[:], results[plane][:].indirect(entries(lists[r], first, count)))
                bank = fw_psum.tile([P, 4, P], F32, name="fw_bank")
                for chunk in range(count // P):
                    nc.tensor.transpose(bank[:, chunk, :], got[:, P * chunk : P * (chunk + 1)], ident[:])
                if r == 1 and between is not None:
                    between()
                for chunk in range(count // P):
                    col = 8 * step + 4 * r + first // P + chunk
                    nc.scalar.activation(
                        gated[:, r, P * chunk : P * (chunk + 1)],
                        bank[:, chunk, :],
                        COPY,
                        scale=gate_cols[:, col : col + 1],
                    )
            return gated

        def turn_back(gated, chunks, dst):
            for n, chunk in enumerate(chunks):
                for r in range(2):
                    nc.tensor.matmul(
                        dst[:, P * n : P * (n + 1)],
                        gated[:, r, P * chunk : P * (chunk + 1)],
                        ident[:],
                        start=(r == 0),
                        stop=(r == 1),
                        is_transpose=True,
                    )

        def combine_turned(step, results, lists, units, finish, late):
            between, after = None, []
            empty_late(step, results, late, 2, ("w_bf3", "pairs512")[step])
            for n, (plane, first, count) in enumerate(units):
                gated = fetch_and_gate(step, results, lists, plane, first, count, between)
                if n == 1:
                    empty_late(step, results, late, 3, "got%d0%d_%d" % (step, plane, first))
                for copy_out in after:
                    copy_out("got%d1%d_%d" % (step, plane, first))
                after = []
                between = partial(finish, plane, first, count, gated, after)
            between()
            for copy_out in after:
                copy_out("gated%d%d_%d" % (step, plane, first))

        def gated_product(dst, window, lst, gates, first, count):
            nc.vector.tensor_tensor(dst, window[:].indirect(entries(lst, first, count)), gates, MULT)

        summed, c_pairs = {}, {}

        def round_c(u, first, count, bank, tag):
            if u not in c_pairs:
                c_pairs[u] = keep.tile([P, T, 2], BF16, name="c_pairs%d" % u, tag=tag, align_bytes=64)
            nc.scalar.copy(c_pairs[u][:, first : first + count, :], bank[:, :, 0:count].rearrange("p b t -> p t b"))

        def sum_c(plane, first, count, gated, after):
            u, b = divmod(plane, 2)
            for at in range(0, count, 256):
                width = min(256, count - at)
                if b == 0:
                    summed[first + at] = acc_psum.tile([P, 2, 256], F32, name="acc_bank")
                turn_back(gated, range(at // P, (at + width) // P), summed[first + at][:, b, :])
                if b == 1:
                    after.append(partial(round_c, u, first + at, width, summed[first + at]))

        combine_turned(0, y, (pos1_sb, pos2_sb), UNITS1, sum_c, late)
        count = T - PLAIN1
        prods = [keep.tile([P, 2, count], F32, name="prod0%d" % r) for r in range(2)]
        for b in range(2):
            for r, lst in enumerate((pos1_sb, pos2_sb)):
                got = keep.tile([P, count], F32, name="plain%d%d" % (r, b))
                nc.vector.tensor_copy(got[:], y[2 + b][:].indirect(entries(lst, PLAIN1, count)))
                nc.gpsimd.tensor_tensor(prods[r][:, b, :], got[:], wide1[:, r, :], MULT)
        nc.vector.tensor_tensor(
            c_pairs[1][:, PLAIN1:T, :].rearrange("p (c i) b -> p c b i", i=4),
            prods[0][:].rearrange("p b (c i) -> p c b i", i=4),
            prods[1][:].rearrange("p b (c i) -> p c b i", i=4),
            ADD,
        )
        c_words = [c_pairs[u][:].rearrange("p t b -> p (t b)").bitcast(U32) for u in range(2)]

        z = [keep.tile([P, S], F32, name="z%d" % j) for j in range(2)]
        c_codes, c_sc, woven, pairs = {}, {}, {}, {}

        def fetch_pairs(first, count, u):
            if u == 0:
                name = "pairs%d" % first
                pairs[first] = keep.tile([P, 2, count], U32, name=name, tag=name, align_bytes=64)
            nc.vector.tensor_copy(pairs[first][:, u, :], c_words[u].indirect(entries(offs2_sb, first, count)))

        def weave(first, count):
            name = "woven%d" % first
            woven[first] = keep.tile([P, count, 2], U32, name=name, tag=name, align_bytes=64)
            nc.scalar.copy(woven[first][:].bitcast(F32), pairs[first][:].bitcast(F32).rearrange("p u s -> p s u"))

        def fetch_woven(first, count, u, tag):
            if first not in woven:
                woven[first] = keep.tile([P, count, 2], U32, name="woven%d" % first, tag=tag, align_bytes=64)
            nc.vector.tensor_copy(woven[first][:, :, u], c_words[u].indirect(entries(offs2_sb, first, count)))

        def quantize_slots(first, count, tag=None):
            name = "c_codes%d" % first
            c_codes[first] = keep.tile([P, count], U32, name=name, tag=tag or name, align_bytes=64)
            c_sc[first] = keep.tile([P, count], U8, name="c_sc%d" % first, align_bytes=64)
            nc.vector.quantize_mx(
                c_codes[first][:].bitcast(FP8X4),
                c_sc[first][:],
                woven[first][:].rearrange("p s u -> p (s u)").bitcast(BF16),
            )
            if first < LAST * C:
                bank = multiply(first // C, 0, c_codes[first][:], c_sc[first][:], count)
                empty(bank, 0, first, count, z)
            else:
                for b in range(2):
                    dst = banks[b][:, first - LAST * C : first - LAST * C + count]
                    one_plane(dst, LAST, b, c_codes[first][:], c_sc[first][:])

        for first in (0, 256, 512):
            fetch_pairs(first, 256, 0)
        fetch_pairs(768, P, 0)
        for first in (0, 256, 512):
            fetch_pairs(first, 256, 1)
            weave(first, 256)
        fetch_pairs(768, P, 1)
        weave(768, P)
        quantize_slots(0, 256)
        quantize_slots(256, 256)
        quantize_slots(512, 256)
        for u in range(2):
            fetch_woven(896, P, u, "pairs512")
        banks = [fw_psum.tile([P, C], F32, name="fw_bank") for b in range(2)]
        quantize_slots(768, P)
        quantize_slots(896, P)
        nc.vector.tensor_copy(z[0][:, LAST * C : S], banks[0][:])
        nc.scalar.copy(z[1][:, LAST * C : S], banks[1][:])
        tokens2 = [(first, count, c_codes[first][:], c_sc[first][:]) for first, count in ((0, 256), (256, 256), (512, 256), (768, P), (896, P))]
        late = [late_banks(half, tokens2) for half in range(2)]

        out_planes = out.rearrange("(p j) t -> p j t", j=4)

        def copy_and_store(plane, src, first, count, tag):
            staged = keep.tile([P, count], F32, name="staged%d_%d" % (plane, first), tag=tag, align_bytes=64)
            nc.scalar.copy(staged[:], src[:, 0:count])
            nc.scalar.dma_start(out_planes[:, plane, first : first + count], staged[:])

        def store(plane, first, count, gated, after):
            bank = acc_psum.tile([P, 2, 256], F32, name="acc_bank")
            flat = bank[:].rearrange("p b t -> p (b t)")
            turn_back(gated, range(count // P), flat)
            after.append(partial(copy_and_store, plane, flat, first, count))

        combine_turned(1, z, (pos3_sb, pos4_sb), UNITS2, store, late)
        count = T - PLAIN2
        prod3 = keep.tile([P, count], F32, name="prod3")
        gated_product(prod3[:], z[3], pos3_sb, wide2[:, 0, :], PLAIN2, count)
        prod4 = keep.tile([P, count], F32, name="prod4")
        halves = [slice(0, count // 2), slice(count // 2, count)]
        for half in halves:
            gated_product(prod4[:, half], z[3], pos4_sb, wide2[:, 1, half], PLAIN2 + half.start, count // 2)
        for half in halves:
            total = keep.tile([P, count // 2], F32, name="total%d" % half.start)
            nc.vector.tensor_tensor(total[:], prod3[:, half], prod4[:, half], ADD)
            nc.sync.dma_start(out_planes[:, 3, PLAIN2 + half.start : PLAIN2 + half.stop], total[:])
